import numpy as np
import ml_dtypes


def mxq(x, axis, fmt="e4m3"):
    dtype, down = {"e4m3": (ml_dtypes.float8_e4m3fn, 7), "e5m2": (ml_dtypes.float8_e5m2, 14)}[fmt]
    v = np.moveaxis(np.asarray(x, np.float32).astype(ml_dtypes.bfloat16).astype(np.float64), axis, -1)
    blocks = v.reshape(v.shape[:-1] + (-1, 32))
    amax = np.abs(blocks).max(-1, keepdims=True)
    byte = np.maximum(np.where(amax > 0, np.frexp(amax)[1] - 1 + 127, 0) - down, 1)
    scale = np.exp2(byte - 127.0)
    codes = (blocks / scale).astype(np.float32).astype(dtype).astype(np.float64)
    return np.moveaxis((codes * scale).reshape(v.shape), -1, axis)


WIDE = False


def mx_kscale(k):
    if not WIDE:
        return np.ones(k)
    levels = np.array([10, -10, 5, -5, 0])
    if k % 512:
        return np.exp2(np.random.permutation(np.resize(levels, k // 32))).repeat(32)
    a = np.empty((k // 512, 16))
    for p in range(k // 512):
        a[p, :8] = np.random.permutation(np.resize(levels, 8))
        for g in range(8):
            far = levels[np.abs(levels - a[p, g]) >= 10]
            a[p, g + 8] = far[np.random.randint(len(far))]
    return np.exp2(a.ravel()).repeat(32)


def f64(x):
    return np.asarray(x).astype(np.float64)


def striped8(idx):
    return np.concatenate([v.reshape(-1, 16).T for v in idx]).astype(np.uint16)


def unstriped8(offs):
    return np.stack([offs[16 * g:16 * g + 16].T.reshape(-1) for g in range(8)]).astype(np.int64)


def split(x):
    m, e = np.frexp(f64(x))
    hi = np.ldexp(np.trunc(16.0 * m) / 16.0, e)
    return hi, f64(x) - hi


K, M, T, S = 512, 1024, 1024, 512


def setup_inputs():
    n = np.random.standard_normal
    s = mx_kscale(K)[:, None]
    return {
        "xT": (n((K, T)) * s).astype(np.float32),
        "w": (n((K, M)) / np.sqrt(K) / s).astype(np.float32),
        "wgt": np.repeat(np.random.uniform(0.5, 2.0, (8, S)), 16, axis=0).astype(np.float32),
        "r": (n((512, 1024))).astype(np.float32),
        "offs": striped8(np.stack([np.random.permutation(T)[:S] for _ in range(8)])),
    }


def reference(xT, w, wgt, r, offs):
    idx = unstriped8(offs)
    group = np.arange(K) % 512 // 64
    xg = f64(wgt)[np.arange(K) // 4 % 128] * f64(xT)[np.arange(K)[:, None], idx[group]]
    xT_ = mxq(xg, 0, "e4m3")
    w_hi, w_lo = split(w)
    w_hi_, w_lo_ = mxq(w_hi, 0, "e4m3"), mxq(w_lo, 0, "e4m3")
    y = xT_.T @ w_hi_ + xT_.T @ w_lo_
    return f64(r) + y

@@ -1,0 +1,166 @@
+from contextlib import ExitStack
+
+import concourse.mybir as mybir
+
+K, M, T, S = 512, 1024, 1024, 512
+FLOPS = 2 * 2 * K * M * S
+
+F32 = mybir.dt.float32
+BF16 = mybir.dt.bfloat16
+I32 = mybir.dt.int32
+U32 = mybir.dt.uint32
+U16 = mybir.dt.uint16
+U8 = mybir.dt.uint8
+FP8X4 = mybir.dt.float8_e4m3fn_x4
+ALU = mybir.AluOpType
+
+P = 128
+PACK = 4
+HI_MASK = -0x000F0010
+
+
+def tile_list_heads_tm_hl_res_kernel(tc, xT, w, wgt, r, offs, out):
+    nc = tc.nc
+    xT_v = xT.rearrange("(p t) w -> p t w", t=PACK)
+    w_v = w.rearrange("(p t) n -> p t n", t=PACK)
+    r_v = r.rearrange("(j p) n -> p j n", p=P)
+
+    with ExitStack() as ctx:
+        lists = ctx.enter_context(tc.tile_pool(name="lists", bufs=1))
+        keep = ctx.enter_context(tc.tile_pool(name="keep", bufs=1))
+        psum = ctx.enter_context(tc.psum_pool(name="psum", bufs=1))
+
+        offsets = lists.tile([P, S // 16], U16, name="offsets")
+        nc.sync.dma_start(offsets[:], offs)
+
+        wgt_t = keep.tile([P, S], F32, name="wgt_t")
+        planes = [keep.tile([P, T], F32, name=f"plane{t}") for t in range(PACK)]
+        WC = 256
+        NCH = M // WC
+        w_raw = [keep.tile([P, PACK, WC], F32, name=f"w_raw{c}") for c in range(NCH)]
+        r_t = [keep.tile([P, S // P, 512], F32, name=f"r_t{h}") for h in range(2)]
+        JH = S // 2
+
+        nc.sync.dma_start(wgt_t[:, 0:JH], wgt[:, 0:JH])
+        nc.sync.dma_start(planes[0][:], xT_v[:, 0, :])
+        nc.sync.dma_start(wgt_t[:, JH:S], wgt[:, JH:S])
+        for t in range(1, PACK):
+            nc.sync.dma_start(planes[t][:], xT_v[:, t, :])
+        nc.sync.dma_start(w_raw[0][:], w_v[:, :, 0:WC])
+        nc.sync.dma_start(w_raw[1][:], w_v[:, :, WC : 2 * WC])
+        nc.sync.dma_start(w_raw[2][:], w_v[:, :, 2 * WC : 3 * WC])
+        nc.sync.dma_start(r_t[0][:], r_v[:, :, 0:512])
+        nc.sync.dma_start(w_raw[3][:], w_v[:, :, 3 * WC : 4 * WC])
+        nc.sync.dma_start(r_t[1][:], r_v[:, :, 512:1024])
+
+        xg = [keep.tile([P, PACK, JH], F32, name=f"xg{h}") for h in range(2)]
+        xb = [keep.tile([P, JH, PACK], BF16, name=f"xb{h}", align_bytes=64) for h in range(2)]
+        x_codes = [keep.tile([P, JH], U32, name=f"x_codes{h}", align_bytes=64) for h in range(2)]
+        x_scales = [keep.tile([P, JH], U8, name=f"x_scales{h}", align_bytes=64) for h in range(2)]
+
+        w_tr = [keep.tile([P, WC, PACK], BF16, name=f"w_tr{c}", align_bytes=64) for c in range(NCH)]
+        w_hi = [keep.tile([P, WC, PACK], BF16, name=f"w_hi{c}", align_bytes=64) for c in range(NCH)]
+        w_lo = [keep.tile([P, WC, PACK], BF16, name=f"w_lo{c}", align_bytes=64) for c in range(NCH)]
+        codes = [[keep.tile([P, 512], U32, name=f"codes{h}_{e}", align_bytes=64) for e in range(2)] for h in range(2)]
+        scales = [[keep.tile([P, 512], U8, name=f"scales{h}_{e}", align_bytes=64) for e in range(2)] for h in range(2)]
+        acc = [[psum.tile([P, 512], F32, name=f"acc{h}_{j}") for j in range(4)] for h in range(2)]
+        res = [[keep.tile([P, 512], F32, name=f"res{h}_{j}") for j in range(4)] for h in range(2)]
+
+        def gather(t, h):
+            nc.vector.tensor_tensor(
+                xg[h][:, t, :],
+                planes[t][:].indirect(offsets[:, h * (JH // 16) : (h + 1) * (JH // 16)]),
+                wgt_t[:, h * JH : (h + 1) * JH],
+                ALU.mult,
+            )
+
+        def by4(tile):
+            return tile[:].rearrange("p (c i) t -> p c t i", i=4)
+
+        def interleave_x(h, copy):
+            copy(out=by4(xb[h]), in_=xg[h][:].rearrange("p t (c i) -> p c t i", i=4))
+
+        def quantize_x(h):
+            nc.vector.quantize_mx(out=x_codes[h][:].bitcast(FP8X4), scales=x_scales[h][:], in_=xb[h][:].rearrange("p j t -> p (j t)"))
+
+        def truncate_w(c):
+            halves = w_raw[c][:].rearrange("p t n -> p (t n)").bitcast(BF16)
+            halves = halves.rearrange("p (t c i h) -> p c t i h", t=PACK, i=4, h=2)
+            nc.scalar.copy(out=by4(w_tr[c]), in_=halves[:, :, :, :, 1])
+
+        def mask_hi(c):
+            nc.vector.tensor_scalar(
+                w_hi[c][:].rearrange("p n t -> p (n t)").bitcast(I32),
+                w_tr[c][:].rearrange("p n t -> p (n t)").bitcast(I32),
+                HI_MASK,
+                None,
+                op0=ALU.bitwise_and,
+            )
+
+        def subtract_lo(c):
+            nc.vector.tensor_tensor(
+                by4(w_lo[c]), w_raw[c][:].rearrange("p t (c i) -> p c t i", i=4), by4(w_hi[c]), ALU.subtract
+            )
+
+        def quantize_w(c, e):
+            src = (w_hi, w_lo)[e][c]
+            h, n0 = c // 2, (c % 2) * WC
+            nc.vector.quantize_mx(
+                out=codes[h][e][:, n0 : n0 + WC].bitcast(FP8X4),
+                scales=scales[h][e][:, n0 : n0 + WC],
+                in_=src[:].rearrange("p n t -> p (n t)"),
+            )
+
+        def multiply(h, e):
+            for j in range(4):
+                q, j0 = j // 2, (j % 2) * P
+                nc.tensor.matmul_mx(
+                    out=acc[h][j][:],
+                    lhsT=x_codes[q][:, j0 : j0 + P].bitcast(FP8X4),
+                    lhsT_scale=x_scales[q][:, j0 : j0 + P],
+                    rhs=codes[h][e][:].bitcast(FP8X4),
+                    rhs_scale=scales[h][e][:],
+                    start=(e == 0),
+                    stop=(e == 1),
+                )
+
+        def finish(h, j):
+            nc.vector.tensor_tensor(res[h][j][:], acc[h][j][:], r_t[h][:, j, :], ALU.add)
+            nc.sync.dma_start(out[j * P : (j + 1) * P, h * 512 : (h + 1) * 512], res[h][j][:])
+
+        for t in range(PACK):
+            gather(t, 0)
+            gather(t, 1)
+        truncate_w(0)
+        interleave_x(0, nc.vector.tensor_copy)
+        mask_hi(0)
+        truncate_w(1)
+        interleave_x(1, nc.scalar.copy)
+        quantize_x(0)
+        subtract_lo(0)
+        mask_hi(1)
+        quantize_w(0, 0)
+        truncate_w(2)
+        subtract_lo(1)
+        quantize_w(0, 1)
+        quantize_x(1)
+        quantize_w(1, 0)
+        mask_hi(2)
+        truncate_w(3)
+        quantize_w(1, 1)
+        multiply(0, 0)
+        multiply(0, 1)
+        subtract_lo(2)
+        mask_hi(3)
+        quantize_w(2, 0)
+        subtract_lo(3)
+        quantize_w(2, 1)
+        quantize_w(3, 0)
+        multiply(1, 0)
+        finish(0, 0)
+        quantize_w(3, 1)
+        multiply(1, 1)
+        for j in range(1, 4):
+            finish(0, j)
+        for j in range(4):
+            finish(1, j)

@@ -16,11 +16,16 @@ ALU = mybir.AluOpType
 
 P = 128
 PACK = 4
+WC = 256
+JH = S // 2
+NB = 512
 HI_MASK = -0x000F0010
+HI_RAW_MASK = -0x00100000
 
 
 def tile_list_heads_tm_hl_res_kernel(tc, xT, w, wgt, r, offs, out):
     nc = tc.nc
+    V, G = nc.vector, nc.gpsimd
     xT_v = xT.rearrange("(p t) w -> p t w", t=PACK)
     w_v = w.rearrange("(p t) n -> p t n", t=PACK)
     r_v = r.rearrange("(j p) n -> p j n", p=P)
@@ -31,136 +36,150 @@ def tile_list_heads_tm_hl_res_kernel(tc, xT, w, wgt, r, offs, out):
         psum = ctx.enter_context(tc.psum_pool(name="psum", bufs=1))
 
         offsets = lists.tile([P, S // 16], U16, name="offsets")
-        nc.sync.dma_start(offsets[:], offs)
-
         wgt_t = keep.tile([P, S], F32, name="wgt_t")
         planes = [keep.tile([P, T], F32, name=f"plane{t}") for t in range(PACK)]
-        WC = 256
-        NCH = M // WC
-        w_raw = [keep.tile([P, PACK, WC], F32, name=f"w_raw{c}") for c in range(NCH)]
-        r_t = [keep.tile([P, S // P, 512], F32, name=f"r_t{h}") for h in range(2)]
-        JH = S // 2
-
-        nc.sync.dma_start(wgt_t[:, 0:JH], wgt[:, 0:JH])
-        nc.sync.dma_start(planes[0][:], xT_v[:, 0, :])
-        nc.sync.dma_start(wgt_t[:, JH:S], wgt[:, JH:S])
-        for t in range(1, PACK):
-            nc.sync.dma_start(planes[t][:], xT_v[:, t, :])
-        nc.sync.dma_start(w_raw[0][:], w_v[:, :, 0:WC])
-        nc.sync.dma_start(w_raw[1][:], w_v[:, :, WC : 2 * WC])
-        nc.sync.dma_start(w_raw[2][:], w_v[:, :, 2 * WC : 3 * WC])
-        nc.sync.dma_start(r_t[0][:], r_v[:, :, 0:512])
-        nc.sync.dma_start(w_raw[3][:], w_v[:, :, 3 * WC : 4 * WC])
-        nc.sync.dma_start(r_t[1][:], r_v[:, :, 512:1024])
-
+        w_t = [keep.tile([P, PACK, WC], F32, name=f"w_t{c}") for c in range(4)]
+        r_t = [keep.tile([P, S // P, NB], F32, name=f"r_t{h}") for h in range(2)]
         xg = [keep.tile([P, PACK, JH], F32, name=f"xg{h}") for h in range(2)]
-        xb = [keep.tile([P, JH, PACK], BF16, name=f"xb{h}", align_bytes=64) for h in range(2)]
+
+        def load_w(c):
+            nc.sync.dma_start(w_t[c][:], w_v[:, :, c * WC : (c + 1) * WC])
+
+        load_w(0)
+        nc.sync.dma_start(offsets[:], offs)
+        nc.sync.dma_start(wgt_t[:], wgt)
+        for t in range(PACK):
+            nc.sync.dma_start(planes[t][:], xT_v[:, t, :])
+        for c in range(1, 4):
+            load_w(c)
+        for h in range(2):
+            nc.sync.dma_start(r_t[h][:], r_v[:, :, h * NB : (h + 1) * NB])
+
         x_codes = [keep.tile([P, JH], U32, name=f"x_codes{h}", align_bytes=64) for h in range(2)]
         x_scales = [keep.tile([P, JH], U8, name=f"x_scales{h}", align_bytes=64) for h in range(2)]
+        w_tr = [keep.tile([P, WC, PACK], BF16, name=f"w_tr{c}", align_bytes=64) for c in range(1, 4)]
+        w_hi = [keep.tile([P, WC, PACK], BF16, name=f"w_hi{c}", align_bytes=64) for c in range(4)]
+        w_lo = [keep.tile([P, WC, PACK], BF16, name=f"w_lo{c}", align_bytes=64) for c in range(4)]
+        w_hr = keep.tile([P, PACK, WC], F32, name="w_hr")
+        scales = [[keep.tile([P, NB], U8, name=f"scales{h}_{e}", align_bytes=64) for e in range(2)] for h in range(2)]
+        codes = [[keep.tile([P, NB], U32, name=f"codes{h}_{e}", align_bytes=64) for e in range(2)] for h in range(2)]
+        acc = [[psum.tile([P, NB], F32, name=f"acc{h}_{j}") for j in range(4)] for h in range(2)]
+        res = [[keep.tile([P, NB], F32, name=f"res{h}_{j}") for j in range(4)] for h in range(2)]
 
-        w_tr = [keep.tile([P, WC, PACK], BF16, name=f"w_tr{c}", align_bytes=64) for c in range(NCH)]
-        w_hi = [keep.tile([P, WC, PACK], BF16, name=f"w_hi{c}", align_bytes=64) for c in range(NCH)]
-        w_lo = [keep.tile([P, WC, PACK], BF16, name=f"w_lo{c}", align_bytes=64) for c in range(NCH)]
-        codes = [[keep.tile([P, 512], U32, name=f"codes{h}_{e}", align_bytes=64) for e in range(2)] for h in range(2)]
-        scales = [[keep.tile([P, 512], U8, name=f"scales{h}_{e}", align_bytes=64) for e in range(2)] for h in range(2)]
-        acc = [[psum.tile([P, 512], F32, name=f"acc{h}_{j}") for j in range(4)] for h in range(2)]
-        res = [[keep.tile([P, 512], F32, name=f"res{h}_{j}") for j in range(4)] for h in range(2)]
+        def by4(ap):
+            return ap.rearrange("p (c i) t -> p c t i", i=4)
+
+        def planes4(ap):
+            return ap.rearrange("p t (c i) -> p c t i", i=4)
+
+        def flat(ap):
+            return ap.rearrange("p n t -> p (n t)")
+
+        def truncate_w(c):
+            halves = w_t[c][:].rearrange("p t n -> p (t n)").bitcast(BF16)
+            halves = halves.rearrange("p (t n h) -> p t n h", t=PACK, h=2)[:, :, :, 1]
+            nc.scalar.copy(out=by4(w_tr[c - 1][:]), in_=planes4(halves))
+
+        def mask_hi(c):
+            V.tensor_scalar(flat(w_hi[c][:]).bitcast(I32), flat(w_tr[c - 1][:]).bitcast(I32), HI_MASK, None, op0=ALU.bitwise_and)
+
+        def subtract_lo(eng, c):
+            eng.tensor_tensor(by4(w_lo[c][:]), planes4(w_t[c][:]), by4(w_hi[c][:]), ALU.subtract)
+
+        def mask_raw():
+            V.tensor_scalar(w_hr[:].bitcast(I32), w_t[0][:].bitcast(I32), HI_RAW_MASK, None, op0=ALU.bitwise_and)
+
+        def interleave_raw_hi():
+            nc.scalar.copy(out=by4(w_hi[0][:]), in_=planes4(w_hr[:]))
+
+        def subtract_raw():
+            V.tensor_tensor(by4(w_lo[0][:]), planes4(w_t[0][:]), planes4(w_hr[:]), ALU.subtract)
+
+        def quantize(codes_ap, scales_ap, src):
+            V.quantize_mx(out=codes_ap.bitcast(FP8X4), scales=scales_ap, in_=flat(src[:]))
+
+        def quantize_x(h):
+            quantize(x_codes[h][:], x_scales[h][:], xb[h])
+
+        def quantize_w(c, e):
+            h, n0 = c // 2, (c % 2) * WC
+            quantize(codes[h][e][:, n0 : n0 + WC], scales[h][e][:, n0 : n0 + WC], (w_hi, w_lo)[e][c])
+
+        def multiply(c, e, tiles=(0, 1, 2, 3)):
+            h, n0 = c // 2, (c % 2) * WC
+            for j in tiles:
+                q, j0 = j // 2, (j % 2) * P
+                nc.tensor.matmul_mx(
+                    out=acc[h][j][:, n0 : n0 + WC],
+                    lhsT=x_codes[q][:, j0 : j0 + P].bitcast(FP8X4),
+                    lhsT_scale=x_scales[q][:, j0 : j0 + P],
+                    rhs=codes[h][e][:, n0 : n0 + WC].bitcast(FP8X4),
+                    rhs_scale=scales[h][e][:, n0 : n0 + WC],
+                    start=(e == 0),
+                    stop=(e == 1),
+                )
+
+        def rows(h, j):
+            return out[j * P : (j + 1) * P, h * NB : (h + 1) * NB]
+
+        def finish(h, j):
+            V.tensor_tensor(res[h][j][:], acc[h][j][:], r_t[h][:, j, :], ALU.add)
+            nc.sync.dma_start(rows(h, j), res[h][j][:])
 
         def gather(t, h):
-            nc.vector.tensor_tensor(
+            V.tensor_tensor(
                 xg[h][:, t, :],
                 planes[t][:].indirect(offsets[:, h * (JH // 16) : (h + 1) * (JH // 16)]),
                 wgt_t[:, h * JH : (h + 1) * JH],
                 ALU.mult,
             )
 
-        def by4(tile):
-            return tile[:].rearrange("p (c i) t -> p c t i", i=4)
-
         def interleave_x(h, copy):
-            copy(out=by4(xb[h]), in_=xg[h][:].rearrange("p t (c i) -> p c t i", i=4))
+            copy(out=by4(xb[h][:]), in_=planes4(xg[h][:]))
 
-        def quantize_x(h):
-            nc.vector.quantize_mx(out=x_codes[h][:].bitcast(FP8X4), scales=x_scales[h][:], in_=xb[h][:].rearrange("p j t -> p (j t)"))
-
-        def truncate_w(c):
-            halves = w_raw[c][:].rearrange("p t n -> p (t n)").bitcast(BF16)
-            halves = halves.rearrange("p (t c i h) -> p c t i h", t=PACK, i=4, h=2)
-            nc.scalar.copy(out=by4(w_tr[c]), in_=halves[:, :, :, :, 1])
-
-        def mask_hi(c):
-            nc.vector.tensor_scalar(
-                w_hi[c][:].rearrange("p n t -> p (n t)").bitcast(I32),
-                w_tr[c][:].rearrange("p n t -> p (n t)").bitcast(I32),
-                HI_MASK,
-                None,
-                op0=ALU.bitwise_and,
-            )
-
-        def subtract_lo(c):
-            nc.vector.tensor_tensor(
-                by4(w_lo[c]), w_raw[c][:].rearrange("p t (c i) -> p c t i", i=4), by4(w_hi[c]), ALU.subtract
-            )
-
-        def quantize_w(c, e):
-            src = (w_hi, w_lo)[e][c]
-            h, n0 = c // 2, (c % 2) * WC
-            nc.vector.quantize_mx(
-                out=codes[h][e][:, n0 : n0 + WC].bitcast(FP8X4),
-                scales=scales[h][e][:, n0 : n0 + WC],
-                in_=src[:].rearrange("p n t -> p (n t)"),
-            )
-
-        def multiply(h, e):
-            for j in range(4):
-                q, j0 = j // 2, (j % 2) * P
-                nc.tensor.matmul_mx(
-                    out=acc[h][j][:],
-                    lhsT=x_codes[q][:, j0 : j0 + P].bitcast(FP8X4),
-                    lhsT_scale=x_scales[q][:, j0 : j0 + P],
-                    rhs=codes[h][e][:].bitcast(FP8X4),
-                    rhs_scale=scales[h][e][:],
-                    start=(e == 0),
-                    stop=(e == 1),
-                )
-
-        def finish(h, j):
-            nc.vector.tensor_tensor(res[h][j][:], acc[h][j][:], r_t[h][:, j, :], ALU.add)
-            nc.sync.dma_start(out[j * P : (j + 1) * P, h * 512 : (h + 1) * 512], res[h][j][:])
-
-        for t in range(PACK):
-            gather(t, 0)
-            gather(t, 1)
-        truncate_w(0)
-        interleave_x(0, nc.vector.tensor_copy)
-        mask_hi(0)
-        truncate_w(1)
-        interleave_x(1, nc.scalar.copy)
-        quantize_x(0)
-        subtract_lo(0)
-        mask_hi(1)
-        quantize_w(0, 0)
-        truncate_w(2)
-        subtract_lo(1)
+        xb = [keep.tile([P, JH, PACK], BF16, name="xb0", align_bytes=64)]
+        mask_raw()
+        interleave_raw_hi()
+        subtract_raw()
+        gather(0, 0)
         quantize_w(0, 1)
-        quantize_x(1)
-        quantize_w(1, 0)
+        gather(0, 1)
+        quantize_w(0, 0)
+        for t in range(1, PACK):
+            for h in range(2):
+                gather(t, h)
+        truncate_w(1)
+        interleave_x(0, V.tensor_copy)
+        truncate_w(2)
+        mask_hi(1)
+        xb.append(keep.tile([P, JH, PACK], BF16, name="xb1", tag="w_tr1", align_bytes=64))
+        quantize_x(0)
+        for e in range(2):
+            multiply(0, e, (0, 1))
+        interleave_x(1, nc.scalar.copy)
+        subtract_lo(V, 1)
         mask_hi(2)
         truncate_w(3)
-        quantize_w(1, 1)
-        multiply(0, 0)
-        multiply(0, 1)
-        subtract_lo(2)
-        mask_hi(3)
+        quantize_w(1, 0)
+        quantize_x(1)
+        for e in range(2):
+            multiply(0, e, (2, 3))
         quantize_w(2, 0)
-        subtract_lo(3)
+        quantize_w(1, 1)
+        for j in range(4):
+            for e in range(2):
+                multiply(1, e, (j,))
+        subtract_lo(V, 2)
+        multiply(2, 0)
+        mask_hi(3)
         quantize_w(2, 1)
+        multiply(2, 1)
         quantize_w(3, 0)
-        multiply(1, 0)
-        finish(0, 0)
-        quantize_w(3, 1)
-        multiply(1, 1)
-        for j in range(1, 4):
+        multiply(3, 0)
+        subtract_lo(G, 3)
+        for j in range(4):
             finish(0, j)
+        quantize_w(3, 1)
+        multiply(3, 1)
         for j in range(4):
             finish(1, j)

@@ -39,7 +39,7 @@ def tile_list_heads_tm_hl_res_kernel(tc, xT, w, wgt, r, offs, out):
         wgt_t = keep.tile([P, S], F32, name="wgt_t")
         planes = [keep.tile([P, T], F32, name=f"plane{t}") for t in range(PACK)]
         w_t = [keep.tile([P, PACK, WC], F32, name=f"w_t{c}") for c in range(4)]
-        r_t = [keep.tile([P, S // P, NB], F32, name=f"r_t{h}") for h in range(2)]
+        r_t = [keep.tile([P, S // P, NB], F32, name=f"r_t{h}", tag=f"r_t{h}", align_bytes=64) for h in range(2)]
         xg = [keep.tile([P, PACK, JH], F32, name=f"xg{h}") for h in range(2)]
 
         def load_w(c):
@@ -49,22 +49,27 @@ def tile_list_heads_tm_hl_res_kernel(tc, xT, w, wgt, r, offs, out):
         nc.sync.dma_start(offsets[:], offs)
         nc.sync.dma_start(wgt_t[:], wgt)
         for t in range(PACK):
+            if t == PACK - 1:
+                load_w(1)
             nc.sync.dma_start(planes[t][:], xT_v[:, t, :])
-        for c in range(1, 4):
-            load_w(c)
+        load_w(2)
+        load_w(3)
         for h in range(2):
             nc.sync.dma_start(r_t[h][:], r_v[:, :, h * NB : (h + 1) * NB])
 
         x_codes = [keep.tile([P, JH], U32, name=f"x_codes{h}", align_bytes=64) for h in range(2)]
         x_scales = [keep.tile([P, JH], U8, name=f"x_scales{h}", align_bytes=64) for h in range(2)]
-        w_tr = [keep.tile([P, WC, PACK], BF16, name=f"w_tr{c}", align_bytes=64) for c in range(1, 4)]
-        w_hi = [keep.tile([P, WC, PACK], BF16, name=f"w_hi{c}", align_bytes=64) for c in range(4)]
-        w_lo = [keep.tile([P, WC, PACK], BF16, name=f"w_lo{c}", align_bytes=64) for c in range(4)]
+        def grouped(name, tag=None):
+            return keep.tile([P, WC, PACK], BF16, name=name, tag=tag or name, align_bytes=64)
+
+        w_tr = [grouped(f"w_tr{c}") for c in range(1, 4)]
+        w_hi = [grouped(f"w_hi{c}") for c in range(4)]
+        w_lo = [grouped(f"w_lo{c}") for c in range(3)]
         w_hr = keep.tile([P, PACK, WC], F32, name="w_hr")
-        scales = [[keep.tile([P, NB], U8, name=f"scales{h}_{e}", align_bytes=64) for e in range(2)] for h in range(2)]
-        codes = [[keep.tile([P, NB], U32, name=f"codes{h}_{e}", align_bytes=64) for e in range(2)] for h in range(2)]
-        acc = [[psum.tile([P, NB], F32, name=f"acc{h}_{j}") for j in range(4)] for h in range(2)]
-        res = [[keep.tile([P, NB], F32, name=f"res{h}_{j}") for j in range(4)] for h in range(2)]
+        scales = [[keep.tile([P, WC], U8, name=f"scales{c}_{e}", align_bytes=64) for e in range(2)] for c in range(4)]
+        codes = [[keep.tile([P, WC], U32, name=f"codes{c}_{e}", align_bytes=64)[:] for e in range(2)] for c in range(3)]
+        acc = [psum.tile([P, 2, WC], F32, name=f"acc{b}") for b in range(8)]
+        res = [keep.tile([P, 2, WC], F32, name=f"res{b}") for b in range(8)]
 
         def by4(ap):
             return ap.rearrange("p (c i) t -> p c t i", i=4)
@@ -102,29 +107,39 @@ def tile_list_heads_tm_hl_res_kernel(tc, xT, w, wgt, r, offs, out):
             quantize(x_codes[h][:], x_scales[h][:], xb[h])
 
         def quantize_w(c, e):
-            h, n0 = c // 2, (c % 2) * WC
-            quantize(codes[h][e][:, n0 : n0 + WC], scales[h][e][:, n0 : n0 + WC], (w_hi, w_lo)[e][c])
+            quantize(codes[c][e], scales[c][e][:], (w_hi, w_lo)[e][c])
 
-        def multiply(c, e, tiles=(0, 1, 2, 3)):
-            h, n0 = c // 2, (c % 2) * WC
+        def bank(c, j):
+            if c < 2:
+                return acc[j][:, c, :]
+            return acc[2 * c + j // 2][:, j % 2, :]
+
+        def multiply(c, tiles):
             for j in tiles:
                 q, j0 = j // 2, (j % 2) * P
-                nc.tensor.matmul_mx(
-                    out=acc[h][j][:, n0 : n0 + WC],
-                    lhsT=x_codes[q][:, j0 : j0 + P].bitcast(FP8X4),
-                    lhsT_scale=x_scales[q][:, j0 : j0 + P],
-                    rhs=codes[h][e][:, n0 : n0 + WC].bitcast(FP8X4),
-                    rhs_scale=scales[h][e][:, n0 : n0 + WC],
-                    start=(e == 0),
-                    stop=(e == 1),
-                )
+                for e in range(2):
+                    nc.tensor.matmul_mx(
+                        out=bank(c, j),
+                        lhsT=x_codes[q][:, j0 : j0 + P].bitcast(FP8X4),
+                        lhsT_scale=x_scales[q][:, j0 : j0 + P],
+                        rhs=codes[c][e].bitcast(FP8X4),
+                        rhs_scale=scales[c][e][:],
+                        start=(e == 0),
+                        stop=(e == 1),
+                    )
 
-        def rows(h, j):
-            return out[j * P : (j + 1) * P, h * NB : (h + 1) * NB]
+        out_v = out.rearrange("(j p) n -> p j n", p=P)
 
-        def finish(h, j):
-            V.tensor_tensor(res[h][j][:], acc[h][j][:], r_t[h][:, j, :], ALU.add)
-            nc.sync.dma_start(rows(h, j), res[h][j][:])
+        def finish(b):
+            if b < 4:
+                r_b = r_t[0][:, b, :].rearrange("p (c n) -> p c n", c=2)
+                out_b = out[b * P : (b + 1) * P, 0:NB].rearrange("p (c n) -> p c n", c=2)
+            else:
+                c, q = divmod(b - 4, 2)
+                r_b = r_t[1][:, 2 * q : 2 * q + 2, c * WC : (c + 1) * WC]
+                out_b = out_v[:, 2 * q : 2 * q + 2, NB + c * WC : NB + (c + 1) * WC]
+            V.tensor_tensor(res[b][:], acc[b][:], r_b, ALU.add)
+            nc.sync.dma_start(out_b, res[b][:])
 
         def gather(t, h):
             V.tensor_tensor(
@@ -137,49 +152,49 @@ def tile_list_heads_tm_hl_res_kernel(tc, xT, w, wgt, r, offs, out):
         def interleave_x(h, copy):
             copy(out=by4(xb[h][:]), in_=planes4(xg[h][:]))
 
-        xb = [keep.tile([P, JH, PACK], BF16, name="xb0", align_bytes=64)]
+        xb = [grouped("xb0")]
         mask_raw()
         interleave_raw_hi()
         subtract_raw()
-        gather(0, 0)
-        quantize_w(0, 1)
-        gather(0, 1)
-        quantize_w(0, 0)
-        for t in range(1, PACK):
+        for t in range(PACK - 2):
             for h in range(2):
                 gather(t, h)
+        quantize_w(0, 0)
+        for h in range(2):
+            gather(PACK - 2, h)
+        quantize_w(0, 1)
         truncate_w(1)
-        interleave_x(0, V.tensor_copy)
-        truncate_w(2)
+        gather(PACK - 1, 0)
         mask_hi(1)
-        xb.append(keep.tile([P, JH, PACK], BF16, name="xb1", tag="w_tr1", align_bytes=64))
-        quantize_x(0)
-        for e in range(2):
-            multiply(0, e, (0, 1))
-        interleave_x(1, nc.scalar.copy)
+        gather(PACK - 1, 1)
+        interleave_x(0, nc.scalar.copy)
         subtract_lo(V, 1)
-        mask_hi(2)
-        truncate_w(3)
+        truncate_w(2)
         quantize_w(1, 0)
-        quantize_x(1)
-        for e in range(2):
-            multiply(0, e, (2, 3))
-        quantize_w(2, 0)
+        quantize_x(0)
+        truncate_w(3)
+        multiply(0, (0, 1))
+        mask_hi(2)
         quantize_w(1, 1)
-        for j in range(4):
-            for e in range(2):
-                multiply(1, e, (j,))
+        multiply(1, (0, 1))
+        xb.append(grouped("xb1", tag="w_tr2"))
+        interleave_x(1, nc.scalar.copy)
         subtract_lo(V, 2)
-        multiply(2, 0)
-        mask_hi(3)
+        quantize_w(2, 0)
         quantize_w(2, 1)
-        multiply(2, 1)
-        quantize_w(3, 0)
-        multiply(3, 0)
+        multiply(2, (0, 1))
+        mask_hi(3)
+        quantize_x(1)
+        for c in range(3):
+            multiply(c, (2, 3))
+        w_lo.append(grouped("w_lo3", tag="w_tr2"))
         subtract_lo(G, 3)
-        for j in range(4):
-            finish(0, j)
-        quantize_w(3, 1)
-        multiply(3, 1)
-        for j in range(4):
-            finish(1, j)
+        for b in (0, 1, 4, 2, 3):
+            finish(b)
+        late = keep.tile([P, 2, WC], U32, name="late", tag="r_t0", align_bytes=64)
+        codes.append([late[:, e, :] for e in range(2)])
+        for e in range(2):
+            quantize_w(3, e)
+        multiply(3, range(4))
+        for b in (5, 6, 7):
+            finish(b)

@@ -68,8 +68,10 @@ def tile_list_heads_tm_hl_res_kernel(tc, xT, w, wgt, r, offs, out):
         w_hr = keep.tile([P, PACK, WC], F32, name="w_hr")
         scales = [[keep.tile([P, WC], U8, name=f"scales{c}_{e}", align_bytes=64) for e in range(2)] for c in range(4)]
         codes = [[keep.tile([P, WC], U32, name=f"codes{c}_{e}", align_bytes=64)[:] for e in range(2)] for c in range(3)]
-        acc = [psum.tile([P, 2, WC], F32, name=f"acc{b}") for b in range(8)]
-        res = [keep.tile([P, 2, WC], F32, name=f"res{b}") for b in range(8)]
+        acc = [psum.tile([P, 2, WC], F32, name=f"acc{b}", tag=f"acc{b}") for b in range(6)]
+        res = [keep.tile([P, 2, WC], F32, name=f"res{b}") for b in range(6)]
+        acc3 = []
+        res3 = [keep.tile([P, WC], F32, name=f"res3_{j}") for j in range(4)]
 
         def by4(ap):
             return ap.rearrange("p (c i) t -> p c t i", i=4)
@@ -88,8 +90,11 @@ def tile_list_heads_tm_hl_res_kernel(tc, xT, w, wgt, r, offs, out):
         def mask_hi(c):
             V.tensor_scalar(flat(w_hi[c][:]).bitcast(I32), flat(w_tr[c - 1][:]).bitcast(I32), HI_MASK, None, op0=ALU.bitwise_and)
 
-        def subtract_lo(eng, c):
-            eng.tensor_tensor(by4(w_lo[c][:]), planes4(w_t[c][:]), by4(w_hi[c][:]), ALU.subtract)
+        def subtract_lo(c):
+            V.tensor_tensor(by4(w_lo[c][:]), planes4(w_t[c][:]), by4(w_hi[c][:]), ALU.subtract)
+
+        def subtract_lo_gpsimd(c):
+            G.tensor_tensor(w_lo[c][:], w_t[c][:].rearrange("p t n -> p n t"), w_hi[c][:], ALU.subtract)
 
         def mask_raw():
             V.tensor_scalar(w_hr[:].bitcast(I32), w_t[0][:].bitcast(I32), HI_RAW_MASK, None, op0=ALU.bitwise_and)
@@ -112,7 +117,9 @@ def tile_list_heads_tm_hl_res_kernel(tc, xT, w, wgt, r, offs, out):
         def bank(c, j):
             if c < 2:
                 return acc[j][:, c, :]
-            return acc[2 * c + j // 2][:, j % 2, :]
+            if c == 2:
+                return acc[4 + j // 2][:, j % 2, :]
+            return acc3[j][:]
 
         def multiply(c, tiles):
             for j in tiles:
@@ -135,11 +142,15 @@ def tile_list_heads_tm_hl_res_kernel(tc, xT, w, wgt, r, offs, out):
                 r_b = r_t[0][:, b, :].rearrange("p (c n) -> p c n", c=2)
                 out_b = out[b * P : (b + 1) * P, 0:NB].rearrange("p (c n) -> p c n", c=2)
             else:
-                c, q = divmod(b - 4, 2)
-                r_b = r_t[1][:, 2 * q : 2 * q + 2, c * WC : (c + 1) * WC]
-                out_b = out_v[:, 2 * q : 2 * q + 2, NB + c * WC : NB + (c + 1) * WC]
+                q = b - 4
+                r_b = r_t[1][:, 2 * q : 2 * q + 2, 0:WC]
+                out_b = out_v[:, 2 * q : 2 * q + 2, NB : NB + WC]
             V.tensor_tensor(res[b][:], acc[b][:], r_b, ALU.add)
             nc.sync.dma_start(out_b, res[b][:])
+
+        def finish3(j):
+            V.tensor_tensor(res3[j][:], acc3[j][:], r_t[1][:, j, WC:NB], ALU.add)
+            nc.sync.dma_start(out_v[:, j, NB + WC : 2 * NB], res3[j][:])
 
         def gather(t, h):
             V.tensor_tensor(
@@ -168,7 +179,7 @@ def tile_list_heads_tm_hl_res_kernel(tc, xT, w, wgt, r, offs, out):
         mask_hi(1)
         gather(PACK - 1, 1)
         interleave_x(0, nc.scalar.copy)
-        subtract_lo(V, 1)
+        subtract_lo(1)
         truncate_w(2)
         quantize_w(1, 0)
         quantize_x(0)
@@ -179,7 +190,7 @@ def tile_list_heads_tm_hl_res_kernel(tc, xT, w, wgt, r, offs, out):
         multiply(1, (0, 1))
         xb.append(grouped("xb1", tag="w_tr2"))
         interleave_x(1, nc.scalar.copy)
-        subtract_lo(V, 2)
+        subtract_lo(2)
         quantize_w(2, 0)
         quantize_w(2, 1)
         multiply(2, (0, 1))
@@ -188,13 +199,16 @@ def tile_list_heads_tm_hl_res_kernel(tc, xT, w, wgt, r, offs, out):
         for c in range(3):
             multiply(c, (2, 3))
         w_lo.append(grouped("w_lo3", tag="w_tr2"))
-        subtract_lo(G, 3)
+        subtract_lo_gpsimd(3)
         for b in (0, 1, 4, 2, 3):
             finish(b)
         late = keep.tile([P, 2, WC], U32, name="late", tag="r_t0", align_bytes=64)
         codes.append([late[:, e, :] for e in range(2)])
         for e in range(2):
             quantize_w(3, e)
+        for j in range(4):
+            acc3.append(psum.tile([P, WC], F32, name=f"acc3_{j}", tag=f"acc{j}"))
         multiply(3, range(4))
-        for b in (5, 6, 7):
-            finish(b)
+        finish(5)
+        for j in range(4):
+            finish3(j)

from contextlib import ExitStack

import concourse.mybir as mybir

K, M, T, S = 512, 1024, 1024, 512
FLOPS = 2 * 2 * K * M * S

F32 = mybir.dt.float32
BF16 = mybir.dt.bfloat16
I32 = mybir.dt.int32
U32 = mybir.dt.uint32
U16 = mybir.dt.uint16
U8 = mybir.dt.uint8
FP8X4 = mybir.dt.float8_e4m3fn_x4
ALU = mybir.AluOpType

P = 128
PACK = 4
WC = 256
JH = S // 2
NB = 512
HI_MASK = -0x000F0010
HI_RAW_MASK = -0x00100000


def tile_list_heads_tm_hl_res_kernel(tc, xT, w, wgt, r, offs, out):
    nc = tc.nc
    V, G = nc.vector, nc.gpsimd
    xT_v = xT.rearrange("(p t) w -> p t w", t=PACK)
    w_v = w.rearrange("(p t) n -> p t n", t=PACK)
    r_v = r.rearrange("(j p) n -> p j n", p=P)

    with ExitStack() as ctx:
        lists = ctx.enter_context(tc.tile_pool(name="lists", bufs=1))
        keep = ctx.enter_context(tc.tile_pool(name="keep", bufs=1))
        psum = ctx.enter_context(tc.psum_pool(name="psum", bufs=1))

        offsets = lists.tile([P, S // 16], U16, name="offsets")
        wgt_t = keep.tile([P, S], F32, name="wgt_t")
        planes = [keep.tile([P, T], F32, name=f"plane{t}") for t in range(PACK)]
        w_t = [keep.tile([P, PACK, WC], F32, name=f"w_t{c}") for c in range(4)]
        r_t = [keep.tile([P, S // P, NB], F32, name=f"r_t{h}", tag=f"r_t{h}", align_bytes=64) for h in range(2)]
        xg = [keep.tile([P, PACK, JH], F32, name=f"xg{h}") for h in range(2)]

        def load_w(c):
            nc.sync.dma_start(w_t[c][:], w_v[:, :, c * WC : (c + 1) * WC])

        load_w(0)
        nc.sync.dma_start(offsets[:], offs)
        nc.sync.dma_start(wgt_t[:], wgt)
        for t in range(PACK):
            if t == PACK - 1:
                load_w(1)
            nc.sync.dma_start(planes[t][:], xT_v[:, t, :])
        load_w(2)
        load_w(3)
        for h in range(2):
            nc.sync.dma_start(r_t[h][:], r_v[:, :, h * NB : (h + 1) * NB])

        x_codes = [keep.tile([P, JH], U32, name=f"x_codes{h}", align_bytes=64) for h in range(2)]
        x_scales = [keep.tile([P, JH], U8, name=f"x_scales{h}", align_bytes=64) for h in range(2)]
        def grouped(name, tag=None):
            return keep.tile([P, WC, PACK], BF16, name=name, tag=tag or name, align_bytes=64)

        w_tr = [grouped(f"w_tr{c}") for c in range(1, 4)]
        w_hi = [grouped(f"w_hi{c}") for c in range(4)]
        w_lo = [grouped(f"w_lo{c}") for c in range(3)]
        w_hr = keep.tile([P, PACK, WC], F32, name="w_hr")
        scales = [[keep.tile([P, WC], U8, name=f"scales{c}_{e}", align_bytes=64) for e in range(2)] for c in range(4)]
        codes = [[keep.tile([P, WC], U32, name=f"codes{c}_{e}", align_bytes=64)[:] for e in range(2)] for c in range(3)]
        acc = [psum.tile([P, 2, WC], F32, name=f"acc{b}", tag=f"acc{b}") for b in range(6)]
        res = [keep.tile([P, 2, WC], F32, name=f"res{b}") for b in range(6)]
        acc3 = []
        res3 = [keep.tile([P, WC], F32, name=f"res3_{j}") for j in range(4)]

        def by4(ap):
            return ap.rearrange("p (c i) t -> p c t i", i=4)

        def planes4(ap):
            return ap.rearrange("p t (c i) -> p c t i", i=4)

        def flat(ap):
            return ap.rearrange("p n t -> p (n t)")

        def truncate_w(c):
            halves = w_t[c][:].rearrange("p t n -> p (t n)").bitcast(BF16)
            halves = halves.rearrange("p (t n h) -> p t n h", t=PACK, h=2)[:, :, :, 1]
            nc.scalar.copy(out=by4(w_tr[c - 1][:]), in_=planes4(halves))

        def mask_hi(c):
            V.tensor_scalar(flat(w_hi[c][:]).bitcast(I32), flat(w_tr[c - 1][:]).bitcast(I32), HI_MASK, None, op0=ALU.bitwise_and)

        def subtract_lo(c):
            V.tensor_tensor(by4(w_lo[c][:]), planes4(w_t[c][:]), by4(w_hi[c][:]), ALU.subtract)

        def subtract_lo_gpsimd(c):
            G.tensor_tensor(w_lo[c][:], w_t[c][:].rearrange("p t n -> p n t"), w_hi[c][:], ALU.subtract)

        def mask_raw():
            V.tensor_scalar(w_hr[:].bitcast(I32), w_t[0][:].bitcast(I32), HI_RAW_MASK, None, op0=ALU.bitwise_and)

        def interleave_raw_hi():
            nc.scalar.copy(out=by4(w_hi[0][:]), in_=planes4(w_hr[:]))

        def subtract_raw():
            V.tensor_tensor(by4(w_lo[0][:]), planes4(w_t[0][:]), planes4(w_hr[:]), ALU.subtract)

        def quantize(codes_ap, scales_ap, src):
            V.quantize_mx(out=codes_ap.bitcast(FP8X4), scales=scales_ap, in_=flat(src[:]))

        def quantize_x(h):
            quantize(x_codes[h][:], x_scales[h][:], xb[h])

        def quantize_w(c, e):
            quantize(codes[c][e], scales[c][e][:], (w_hi, w_lo)[e][c])

        def bank(c, j):
            if c < 2:
                return acc[j][:, c, :]
            if c == 2:
                return acc[4 + j // 2][:, j % 2, :]
            return acc3[j][:]

        def multiply(c, tiles):
            for j in tiles:
                q, j0 = j // 2, (j % 2) * P
                for e in range(2):
                    nc.tensor.matmul_mx(
                        out=bank(c, j),
                        lhsT=x_codes[q][:, j0 : j0 + P].bitcast(FP8X4),
                        lhsT_scale=x_scales[q][:, j0 : j0 + P],
                        rhs=codes[c][e].bitcast(FP8X4),
                        rhs_scale=scales[c][e][:],
                        start=(e == 0),
                        stop=(e == 1),
                    )

        out_v = out.rearrange("(j p) n -> p j n", p=P)

        def finish(b):
            if b < 4:
                r_b = r_t[0][:, b, :].rearrange("p (c n) -> p c n", c=2)
                out_b = out[b * P : (b + 1) * P, 0:NB].rearrange("p (c n) -> p c n", c=2)
            else:
                q = b - 4
                r_b = r_t[1][:, 2 * q : 2 * q + 2, 0:WC]
                out_b = out_v[:, 2 * q : 2 * q + 2, NB : NB + WC]
            V.tensor_tensor(res[b][:], acc[b][:], r_b, ALU.add)
            nc.sync.dma_start(out_b, res[b][:])

        def finish3(j):
            V.tensor_tensor(res3[j][:], acc3[j][:], r_t[1][:, j, WC:NB], ALU.add)
            nc.sync.dma_start(out_v[:, j, NB + WC : 2 * NB], res3[j][:])

        def gather(t, h):
            V.tensor_tensor(
                xg[h][:, t, :],
                planes[t][:].indirect(offsets[:, h * (JH // 16) : (h + 1) * (JH // 16)]),
                wgt_t[:, h * JH : (h + 1) * JH],
                ALU.mult,
            )

        def interleave_x(h, copy):
            copy(out=by4(xb[h][:]), in_=planes4(xg[h][:]))

        xb = [grouped("xb0")]
        mask_raw()
        interleave_raw_hi()
        subtract_raw()
        for t in range(PACK - 2):
            for h in range(2):
                gather(t, h)
        quantize_w(0, 0)
        for h in range(2):
            gather(PACK - 2, h)
        quantize_w(0, 1)
        truncate_w(1)
        gather(PACK - 1, 0)
        mask_hi(1)
        gather(PACK - 1, 1)
        interleave_x(0, nc.scalar.copy)
        subtract_lo(1)
        truncate_w(2)
        quantize_w(1, 0)
        quantize_x(0)
        truncate_w(3)
        multiply(0, (0, 1))
        mask_hi(2)
        quantize_w(1, 1)
        multiply(1, (0, 1))
        xb.append(grouped("xb1", tag="w_tr2"))
        interleave_x(1, nc.scalar.copy)
        subtract_lo(2)
        quantize_w(2, 0)
        quantize_w(2, 1)
        multiply(2, (0, 1))
        mask_hi(3)
        quantize_x(1)
        for c in range(3):
            multiply(c, (2, 3))
        w_lo.append(grouped("w_lo3", tag="w_tr2"))
        subtract_lo_gpsimd(3)
        for b in (0, 1, 4, 2, 3):
            finish(b)
        late = keep.tile([P, 2, WC], U32, name="late", tag="r_t0", align_bytes=64)
        codes.append([late[:, e, :] for e in range(2)])
        for e in range(2):
            quantize_w(3, e)
        for j in range(4):
            acc3.append(psum.tile([P, WC], F32, name=f"acc3_{j}", tag=f"acc{j}"))
        multiply(3, range(4))
        finish(5)
        for j in range(4):
            finish3(j)
